import numpy as np
import ml_dtypes


def mxq(x, axis, fmt="e4m3"):
    dtype, down = {"e4m3": (ml_dtypes.float8_e4m3fn, 7), "e5m2": (ml_dtypes.float8_e5m2, 14)}[fmt]
    v = np.moveaxis(np.asarray(x, np.float32).astype(ml_dtypes.bfloat16).astype(np.float64), axis, -1)
    blocks = v.reshape(v.shape[:-1] + (-1, 32))
    amax = np.abs(blocks).max(-1, keepdims=True)
    byte = np.maximum(np.where(amax > 0, np.frexp(amax)[1] - 1 + 127, 0) - down, 1)
    scale = np.exp2(byte - 127.0)
    codes = (blocks / scale).astype(np.float32).astype(dtype).astype(np.float64)
    return np.moveaxis((codes * scale).reshape(v.shape), -1, axis)


WIDE = False


def mx_kscale(k):
    if not WIDE:
        return np.ones(k)
    levels = np.array([10, -10, 5, -5, 0])
    if k % 512:
        return np.exp2(np.random.permutation(np.resize(levels, k // 32))).repeat(32)
    a = np.empty((k // 512, 16))
    for p in range(k // 512):
        a[p, :8] = np.random.permutation(np.resize(levels, 8))
        for g in range(8):
            far = levels[np.abs(levels - a[p, g]) >= 10]
            a[p, g + 8] = far[np.random.randint(len(far))]
    return np.exp2(a.ravel()).repeat(32)


def f64(x):
    return np.asarray(x).astype(np.float64)


def striped(idx):
    return np.tile(np.asarray(idx).reshape(-1, 16).T, (8, 1)).astype(np.uint16)


def unstriped(offs):
    return offs[:16].T.reshape(-1).astype(np.int64)


E2M1 = np.array([0.0, 0.5, 1.0, 1.5, 2.0, 3.0, 4.0, 6.0, -0.0, -0.5, -1.0, -1.5, -2.0, -3.0, -4.0, -6.0])


def pack_weight(w, fmt):
    k, n = w.shape
    w = f64(np.asarray(w, np.float32).astype(ml_dtypes.bfloat16)).reshape(k // 32, 32, n)
    amax = np.abs(w).max(1)
    if fmt == "e4m3":
        byte = np.frexp(amax)[1] - 1 + 127 - 7
    else:
        mant, ex = np.frexp(amax / 6.0)
        byte = np.where(mant > 0.5, ex, ex - 1) + 127
    byte = np.clip(np.where(amax > 0, byte, 1), 1, 254)
    scaled = (w * np.exp2(127.0 - byte)[:, None, :]).reshape(k, n).astype(np.float32)
    by_word = np.ascontiguousarray(scaled.reshape(k // 512, 128, 4, n).transpose(0, 1, 3, 2))
    if fmt == "e4m3":
        words = by_word.astype(ml_dtypes.float8_e4m3fn).view(np.uint8)
    else:
        c = by_word.astype(ml_dtypes.float4_e2m1fn).view(np.uint8) & 0xF
        words = (c[..., 0::2] | (c[..., 1::2] << 4)).reshape(k // 512, 128, 2 * n)
    return np.ascontiguousarray(words), np.ascontiguousarray(byte.astype(np.uint8).reshape(k // 512, 16, n))


def unpack_weight(words, scales, fmt):
    g, _, n = scales.shape
    words = np.ascontiguousarray(words).reshape(g, 128, n, -1)
    if fmt == "e4m3":
        vals = words.view(ml_dtypes.float8_e4m3fn).astype(np.float64)
    else:
        nib = np.empty((g, 128, n, 4), np.uint8)
        nib[..., 0::2] = words & 0xF
        nib[..., 1::2] = words >> 4
        vals = E2M1[nib]
    vals = vals * np.repeat(np.exp2(scales.astype(np.float64) - 127.0), 8, axis=1)[..., None]
    return vals.transpose(0, 1, 3, 2).reshape(g * 512, n)


B, N, T, D, NQ = 1, 512, 2048, 1024, 512
SEG = 16


def setup_inputs():
    n = np.random.standard_normal
    idx = np.random.permutation(T)[:B * N]
    s = mx_kscale(D)[:, None]
    kp = pack_weight(n((D, T)) / s, "e2m1")
    return {
        "qT": (n((B, D, NQ)) * s * (1.00 / np.sqrt(D))).astype(np.float32),
        "k_words": np.ascontiguousarray(kp[0].reshape(1, 2, 128, T, 2).transpose(0, 2, 3, 1, 4)).reshape(1, 128, T, 4),
        "k_scales": kp[1],
        "hw": (np.random.uniform(-0.5, 1.0, (B, 1, NQ))).astype(np.float32),
        "offs": striped(idx),
    }


def reference(qT, k_words, k_scales, hw, offs):
    idx = unstriped(offs)
    pick = lambda x, which: x[:, which].reshape(x.shape[0], B, -1).transpose(1, 0, 2)
    k = unpack_weight(k_words.reshape(1, 128, T, 2, 2).transpose(0, 3, 1, 2, 4).reshape(2, 128, 2 * T), k_scales, "e2m1")
    kg = pick(k, idx)
    qq = mxq(f64(qT), 1, "e4m3")
    a = kg.transpose(0, 2, 1) @ qq
    y = np.tanh((a * f64(hw)).reshape(B, N, NQ // SEG, SEG).max(-1))
    return y

@@ -1,0 +1,174 @@
+from contextlib import ExitStack
+
+import concourse.mybir as mybir
+from concourse.masks import make_identity
+
+N, T, D, NQ, SEG = 512, 2048, 1024, 512, 16
+P = 128
+PACK = 4
+PASSES = 2
+HALF = 256
+
+F32 = mybir.dt.float32
+BF16 = mybir.dt.bfloat16
+I32 = mybir.dt.int32
+U32 = mybir.dt.uint32
+U16 = mybir.dt.uint16
+U8 = mybir.dt.uint8
+FP8X4 = mybir.dt.float8_e4m3fn_x4
+FP4X4 = mybir.dt.float4_e2m1fn_x4
+ALU = mybir.AluOpType
+ACT = mybir.ActivationFunctionType
+AX = mybir.AxisListType
+
+FLOPS = 2 * N * NQ * D
+
+
+def tile_attend_tok_headmax_topk_kernel(tc, qT, k_words, k_scales, hw, offs, out):
+    nc = tc.nc
+    with ExitStack() as ctx:
+        sb = ctx.enter_context(tc.tile_pool(name="sb", bufs=1))
+        reused = ctx.enter_context(tc.tile_pool(name="reused", bufs=1))
+        ps = ctx.enter_context(tc.psum_pool(name="ps", bufs=1))
+
+        RAW_BYTES = PACK * HALF * 4
+        offsets = sb.tile([P, N // 16], U16, name="offsets")
+        pool_scales = reused.tile([P, 3 * RAW_BYTES], U8, name="pool_scales", offset=0)
+        pool_words = sb.tile([P, T], U32, name="pool_words", align_bytes=64)
+        hw_row = sb.tile([P, NQ], F32, name="hw_row")
+        raw = {}
+
+        def load_q(c, o, tile):
+            raw[c, o] = tile
+            nc.sync.dma_start(
+                out=tile[:],
+                in_=qT[0, 512 * o : 512 * (o + 1), HALF * c : HALF * (c + 1)].rearrange("(p j) w -> p j w", j=PACK),
+            )
+
+        nc.sync.dma_start(offsets[:], offs)
+        nc.sync.dma_start(
+            out=pool_scales[0:32, 0:T].bitcast(I32),
+            in_=k_scales.bitcast(I32).rearrange("o f t -> f o t"),
+        )
+        nc.sync.dma_start(
+            out=pool_words[:].bitcast(I32),
+            in_=k_words.rearrange("v p t b -> p (v t b)").bitcast(I32),
+        )
+        load_q(0, 0, sb.tile([P, PACK, HALF], F32, name="raw00"))
+
+        warm = sb.tile([P, 1], F32, name="warm")
+        warm_out = sb.tile([P, 1], F32, name="warm_out")
+        nc.gpsimd.memset(warm[:], 0.0)
+        nc.scalar.activation(out=warm_out[:], in_=warm[:], func=ACT.Tanh)
+        nc.gpsimd.memset(pool_scales[32:64, 0:T].bitcast(I32), 0)
+        nc.vector.memset(pool_scales[64:128, 0:T].bitcast(I32), 0)
+        nc.vector.memset(hw_row[:], 0.0)
+        nc.scalar.dma_start(out=hw_row[0:1, :], in_=hw[0])
+        k_planes = sb.tile([P, PASSES, N], U8, name="k_planes", align_bytes=64)
+        nc.gpsimd.memset(k_planes[:].rearrange("p o n -> p (o n)").bitcast(I32), 0)
+        ident = sb.tile([P, P], F32, name="ident")
+        make_identity(nc, ident[:])
+
+        got_scales = sb.tile([P, N], U8, name="got_scales", align_bytes=64)
+        nc.vector.tensor_copy(got_scales[:], pool_scales[:, 0:T].indirect(offsets[:]))
+        for Q in range(4):
+            nc.scalar.dma_start(
+                out=k_planes[32 * Q : 32 * Q + 4, :, :].bitcast(I32),
+                in_=got_scales[8 * Q : 8 * Q + 8, :].bitcast(I32),
+            )
+        for i, (c, o) in enumerate([(0, 1), (1, 0), (1, 1)]):
+            load_q(c, o, reused.tile([P, PACK, HALF], F32, name="raw%d%d" % (c, o), offset=i * RAW_BYTES))
+
+        hw_turned = ps.tile([P, 4, P], F32, name="hw_turned", tag="bank4")
+        for r in range(2):
+            nc.tensor.transpose(hw_turned[:, r, :], hw_row[:, r:HALF:2], ident[:])
+            nc.tensor.transpose(hw_turned[:, 2 + r, :], hw_row[:, HALF + P * r : HALF + P * (r + 1)], ident[:])
+        hw_cols = sb.tile([P, 4], F32, name="hw_cols")
+        nc.scalar.copy(out=hw_cols[:], in_=hw_turned[:, :, 0])
+
+        got_words = sb.tile([P, N], U32, name="got_words", align_bytes=64)
+        nc.vector.tensor_copy(got_words[:], pool_words[:].indirect(offsets[:]))
+        k_codes = []
+        halves = got_words[:].bitcast(U16).rearrange("p (n o) -> p o n", o=PASSES)
+        for o in range(PASSES):
+            k_codes.append(sb.tile([P, N], U16, name="k_codes%d" % o, align_bytes=64))
+            nc.vector.tensor_copy(out=k_codes[o][:], in_=halves[:, o, :])
+
+        def score(c, o, acc, on_vector):
+            grouped = []
+            for r in range(2):
+                g = sb.tile([P, P, PACK], BF16, name="grouped%d%d%d" % (c, o, r), align_bytes=64)
+                grouped.append(g)
+                if c == 0:
+                    src = raw[c, o][:].rearrange("p j (m r) -> p r m j", r=2)[:, r, :, :]
+                else:
+                    src = raw[c, o][:].rearrange("p j (r m) -> p r m j", r=2)[:, r, :, :]
+                v = on_vector[r]
+                if v > 0:
+                    nc.vector.tensor_copy(out=g[:, 0:v, :], in_=src[:, 0:v, :])
+                if v < P:
+                    nc.scalar.copy(out=g[:, v:P, :], in_=src[:, v:P, :])
+            for r in range(2):
+                codes = sb.tile([P, P], U32, name="codes%d%d%d" % (c, o, r), align_bytes=64)
+                scales = sb.tile([P, P], U8, name="scales%d%d%d" % (c, o, r), align_bytes=64)
+                nc.vector.quantize_mx(
+                    out=codes[:].bitcast(FP8X4), scales=scales[:], in_=grouped[r][:].rearrange("p m j -> p (m j)")
+                )
+                nc.tensor.matmul_mx(
+                    out=acc[r][:],
+                    lhsT=codes[:].bitcast(FP8X4),
+                    lhsT_scale=scales[:],
+                    rhs=k_codes[o][:].bitcast(FP4X4),
+                    rhs_scale=k_planes[:, o, :],
+                    start=(o == 0),
+                    stop=(o == PASSES - 1),
+                )
+
+        result = sb.tile([P, 4, NQ // SEG], F32, name="result")
+        acc_a = [ps.tile([P, N], F32, name="acc_a%d" % r, tag="bank%d" % r) for r in range(2)]
+        acc_b = [ps.tile([P, N], F32, name="acc_b%d" % r, tag="bank%d" % (2 + r)) for r in range(2)]
+        score(0, 0, acc_a, [0, 0])
+        score(0, 1, acc_a, [P, 0])
+
+        first = sb.tile([P, 4, P], F32, name="first")
+        nc.scalar.activation(
+            out=first[:], in_=acc_a[0][:].rearrange("p (m s) -> p s m", s=4), func=ACT.Copy, scale=hw_cols[:, 0:1]
+        )
+        score(1, 0, acc_b, [P, 0])
+        both = sb.tile([P, 4, P], F32, name="both")
+        nc.vector.scalar_tensor_tensor(
+            out=both[:],
+            in0=acc_a[1][:].rearrange("p (m s) -> p s m", s=4),
+            scalar=hw_cols[:, 1:2],
+            in1=first[:],
+            op0=ALU.mult,
+            op1=ALU.max,
+        )
+        turned_a = ps.tile([P, 4, P], F32, name="turned_a", tag="bank5")
+        for s in range(4):
+            nc.tensor.transpose(turned_a[:, s, :], both[:, s, :], ident[:])
+        score(1, 1, acc_b, [P, P // 2])
+        best = sb.tile([P, 4, 16], F32, name="best")
+        nc.vector.tensor_reduce(
+            out=best[:], in_=turned_a[:].rearrange("p s (j h) -> p s j h", h=8), axis=AX.X, op=ALU.max
+        )
+
+        for r, s0, s1, bank in [(0, 0, 4, 4), (1, 0, 2, 6), (1, 2, 4, 7)]:
+            squashed = sb.tile([P, s1 - s0, P], F32, name="squashed%d" % bank)
+            nc.scalar.activation(
+                out=squashed[:],
+                in_=acc_b[r][:].rearrange("p (m s) -> p s m", s=4)[:, s0:s1, :],
+                func=ACT.Tanh,
+                scale=hw_cols[:, 2 + r : 3 + r],
+            )
+            turned = ps.tile([P, s1 - s0, P], F32, name="turned%d" % bank, tag="bank%d" % bank)
+            for s in range(s1 - s0):
+                nc.tensor.transpose(turned[:, s, :], squashed[:, s, :], ident[:])
+            nc.vector.tensor_reduce(
+                out=result[:, s0:s1, 16 + 8 * r : 24 + 8 * r],
+                in_=turned[:].rearrange("p s (j h) -> p s j h", h=SEG),
+                axis=AX.X,
+                op=ALU.max,
+            )
+        nc.scalar.activation(out=result[:, :, 0:16], in_=best[:], func=ACT.Tanh)
+        nc.sync.dma_start(out=out[0].rearrange("(m s) j -> m s j", s=4), in_=result[:])

@@ -33,9 +33,9 @@ def tile_attend_tok_headmax_topk_kernel(tc, qT, k_words, k_scales, hw, offs, out
 
         RAW_BYTES = PACK * HALF * 4
         offsets = sb.tile([P, N // 16], U16, name="offsets")
-        pool_scales = reused.tile([P, 3 * RAW_BYTES], U8, name="pool_scales", offset=0)
+        pool_scales = reused.tile([P, 2 * RAW_BYTES], U8, name="pool_scales", offset=0)
         pool_words = sb.tile([P, T], U32, name="pool_words", align_bytes=64)
-        hw_row = sb.tile([P, NQ], F32, name="hw_row")
+        hw_cols = sb.tile([P, 2, 2], F32, name="hw_cols")
         raw = {}
 
         def load_q(c, o, tile):
@@ -45,25 +45,25 @@ def tile_attend_tok_headmax_topk_kernel(tc, qT, k_words, k_scales, hw, offs, out
                 in_=qT[0, 512 * o : 512 * (o + 1), HALF * c : HALF * (c + 1)].rearrange("(p j) w -> p j w", j=PACK),
             )
 
-        nc.sync.dma_start(offsets[:], offs)
         nc.sync.dma_start(
             out=pool_scales[0:32, 0:T].bitcast(I32),
             in_=k_scales.bitcast(I32).rearrange("o f t -> f o t"),
         )
+        nc.sync.dma_start(offsets[:], offs)
         nc.sync.dma_start(
             out=pool_words[:].bitcast(I32),
             in_=k_words.rearrange("v p t b -> p (v t b)").bitcast(I32),
         )
-        load_q(0, 0, sb.tile([P, PACK, HALF], F32, name="raw00"))
+        for o in range(PASSES):
+            load_q(0, o, sb.tile([P, PACK, HALF], F32, name="raw0%d" % o))
+        nc.sync.dma_start(out=hw_cols[:], in_=hw[0, 0, :].rearrange("(c p r) -> p c r", c=2, r=2))
 
+        nc.vector.memset(pool_scales[32:64, 0:T].bitcast(I32), 0)
+        nc.vector.memset(pool_scales[64:128, 0:T].bitcast(I32), 0)
         warm = sb.tile([P, 1], F32, name="warm")
         warm_out = sb.tile([P, 1], F32, name="warm_out")
         nc.gpsimd.memset(warm[:], 0.0)
         nc.scalar.activation(out=warm_out[:], in_=warm[:], func=ACT.Tanh)
-        nc.gpsimd.memset(pool_scales[32:64, 0:T].bitcast(I32), 0)
-        nc.vector.memset(pool_scales[64:128, 0:T].bitcast(I32), 0)
-        nc.vector.memset(hw_row[:], 0.0)
-        nc.scalar.dma_start(out=hw_row[0:1, :], in_=hw[0])
         k_planes = sb.tile([P, PASSES, N], U8, name="k_planes", align_bytes=64)
         nc.gpsimd.memset(k_planes[:].rearrange("p o n -> p (o n)").bitcast(I32), 0)
         ident = sb.tile([P, P], F32, name="ident")
@@ -72,19 +72,12 @@ def tile_attend_tok_headmax_topk_kernel(tc, qT, k_words, k_scales, hw, offs, out
         got_scales = sb.tile([P, N], U8, name="got_scales", align_bytes=64)
         nc.vector.tensor_copy(got_scales[:], pool_scales[:, 0:T].indirect(offsets[:]))
         for Q in range(4):
-            nc.scalar.dma_start(
+            nc.sync.dma_start(
                 out=k_planes[32 * Q : 32 * Q + 4, :, :].bitcast(I32),
                 in_=got_scales[8 * Q : 8 * Q + 8, :].bitcast(I32),
             )
-        for i, (c, o) in enumerate([(0, 1), (1, 0), (1, 1)]):
-            load_q(c, o, reused.tile([P, PACK, HALF], F32, name="raw%d%d" % (c, o), offset=i * RAW_BYTES))
-
-        hw_turned = ps.tile([P, 4, P], F32, name="hw_turned", tag="bank4")
-        for r in range(2):
-            nc.tensor.transpose(hw_turned[:, r, :], hw_row[:, r:HALF:2], ident[:])
-            nc.tensor.transpose(hw_turned[:, 2 + r, :], hw_row[:, HALF + P * r : HALF + P * (r + 1)], ident[:])
-        hw_cols = sb.tile([P, 4], F32, name="hw_cols")
-        nc.scalar.copy(out=hw_cols[:], in_=hw_turned[:, :, 0])
+        for o in range(PASSES):
+            load_q(1, o, reused.tile([P, PACK, HALF], F32, name="raw1%d" % o, offset=o * RAW_BYTES))
 
         got_words = sb.tile([P, N], U32, name="got_words", align_bytes=64)
         nc.vector.tensor_copy(got_words[:], pool_words[:].indirect(offsets[:]))
@@ -94,25 +87,23 @@ def tile_attend_tok_headmax_topk_kernel(tc, qT, k_words, k_scales, hw, offs, out
             k_codes.append(sb.tile([P, N], U16, name="k_codes%d" % o, align_bytes=64))
             nc.vector.tensor_copy(out=k_codes[o][:], in_=halves[:, o, :])
 
-        def score(c, o, acc, on_vector):
-            grouped = []
-            for r in range(2):
-                g = sb.tile([P, P, PACK], BF16, name="grouped%d%d%d" % (c, o, r), align_bytes=64)
-                grouped.append(g)
-                if c == 0:
-                    src = raw[c, o][:].rearrange("p j (m r) -> p r m j", r=2)[:, r, :, :]
-                else:
-                    src = raw[c, o][:].rearrange("p j (r m) -> p r m j", r=2)[:, r, :, :]
-                v = on_vector[r]
-                if v > 0:
-                    nc.vector.tensor_copy(out=g[:, 0:v, :], in_=src[:, 0:v, :])
-                if v < P:
-                    nc.scalar.copy(out=g[:, v:P, :], in_=src[:, v:P, :])
+        def weave(c, o, r, tag, engine):
+            g = sb.tile([P, P, PACK], BF16, name="woven", tag=tag, align_bytes=64)
+            dst = g[:].rearrange("p (n i) j -> p n j i", i=4)
+            src = raw[c, o][:].rearrange("p j (n i r) -> p r n j i", r=2, i=4)[:, r]
+            if engine == "v":
+                nc.vector.tensor_copy(out=dst, in_=src)
+            else:
+                nc.scalar.copy(out=dst, in_=src)
+            return g
+
+        def score(c, o, acc):
+            woven = [weave(c, o, r, [["w0", "w1"], ["w1", "w2"], ["w2", "w3"], ["w3", "w4"]][2 * c + o][r], [["s", "s"], ["v", "s"], ["v", "s"], ["v", "s"]][2 * c + o][r]) for r in range(2)]
             for r in range(2):
                 codes = sb.tile([P, P], U32, name="codes%d%d%d" % (c, o, r), align_bytes=64)
                 scales = sb.tile([P, P], U8, name="scales%d%d%d" % (c, o, r), align_bytes=64)
                 nc.vector.quantize_mx(
-                    out=codes[:].bitcast(FP8X4), scales=scales[:], in_=grouped[r][:].rearrange("p m j -> p (m j)")
+                    out=codes[:].bitcast(FP8X4), scales=scales[:], in_=woven[r][:].rearrange("p m j -> p (m j)")
                 )
                 nc.tensor.matmul_mx(
                     out=acc[r][:],
@@ -124,51 +115,32 @@ def tile_attend_tok_headmax_topk_kernel(tc, qT, k_words, k_scales, hw, offs, out
                     stop=(o == PASSES - 1),
                 )
 
+        acc = [[ps.tile([P, N], F32, name="acc", tag="acc%d%d" % (c, r)) for r in range(2)] for c in range(2)]
+        for c in range(2):
+            for o in range(PASSES):
+                score(c, o, acc[c])
+
+        both = {}
+        for c, s0, s1 in [(0, 0, 4), (1, 0, 2), (1, 2, 4)]:
+            dealt = [acc[c][r][:].rearrange("p (m s) -> p s m", s=4)[:, s0:s1, :] for r in range(2)]
+            first = sb.tile([P, s1 - s0, P], F32, name="first", tag="first%d" % s0)
+            nc.scalar.activation(out=first[:], in_=dealt[0], func=ACT.Copy, scale=hw_cols[:, c, 0:1])
+            larger = sb.tile(
+                [P, s1 - s0, P], F32, name="larger", tag=["w4", "larger10", "larger12"][c + s0 // 2], align_bytes=64
+            )
+            nc.vector.scalar_tensor_tensor(
+                out=larger[:], in0=dealt[1], scalar=hw_cols[:, c, 1:2], in1=first[:], op0=ALU.mult, op1=ALU.max
+            )
+            for s in range(s0, s1):
+                both[c, s] = larger[:, s - s0, :]
         result = sb.tile([P, 4, NQ // SEG], F32, name="result")
-        acc_a = [ps.tile([P, N], F32, name="acc_a%d" % r, tag="bank%d" % r) for r in range(2)]
-        acc_b = [ps.tile([P, N], F32, name="acc_b%d" % r, tag="bank%d" % (2 + r)) for r in range(2)]
-        score(0, 0, acc_a, [0, 0])
-        score(0, 1, acc_a, [P, 0])
-
-        first = sb.tile([P, 4, P], F32, name="first")
-        nc.scalar.activation(
-            out=first[:], in_=acc_a[0][:].rearrange("p (m s) -> p s m", s=4), func=ACT.Copy, scale=hw_cols[:, 0:1]
-        )
-        score(1, 0, acc_b, [P, 0])
-        both = sb.tile([P, 4, P], F32, name="both")
-        nc.vector.scalar_tensor_tensor(
-            out=both[:],
-            in0=acc_a[1][:].rearrange("p (m s) -> p s m", s=4),
-            scalar=hw_cols[:, 1:2],
-            in1=first[:],
-            op0=ALU.mult,
-            op1=ALU.max,
-        )
-        turned_a = ps.tile([P, 4, P], F32, name="turned_a", tag="bank5")
-        for s in range(4):
-            nc.tensor.transpose(turned_a[:, s, :], both[:, s, :], ident[:])
-        score(1, 1, acc_b, [P, P // 2])
-        best = sb.tile([P, 4, 16], F32, name="best")
-        nc.vector.tensor_reduce(
-            out=best[:], in_=turned_a[:].rearrange("p s (j h) -> p s j h", h=8), axis=AX.X, op=ALU.max
-        )
-
-        for r, s0, s1, bank in [(0, 0, 4, 4), (1, 0, 2, 6), (1, 2, 4, 7)]:
-            squashed = sb.tile([P, s1 - s0, P], F32, name="squashed%d" % bank)
-            nc.scalar.activation(
-                out=squashed[:],
-                in_=acc_b[r][:].rearrange("p (m s) -> p s m", s=4)[:, s0:s1, :],
-                func=ACT.Tanh,
-                scale=hw_cols[:, 2 + r : 3 + r],
-            )
-            turned = ps.tile([P, s1 - s0, P], F32, name="turned%d" % bank, tag="bank%d" % bank)
-            for s in range(s1 - s0):
-                nc.tensor.transpose(turned[:, s, :], squashed[:, s, :], ident[:])
+        for c, s0, s1 in [(0, 0, 4), (1, 0, 2), (1, 2, 4)]:
+            best = sb.tile([P, s1 - s0, 16], F32, name="best", tag=["first2", "best10", "best12"][c + s0 // 2])
+            turned = ps.tile([P, s1 - s0, P], F32, name="turned%d%d" % (c, s0))
+            for s in range(s0, s1):
+                nc.tensor.transpose(turned[:, s - s0, :], both[c, s], ident[:])
             nc.vector.tensor_reduce(
-                out=result[:, s0:s1, 16 + 8 * r : 24 + 8 * r],
-                in_=turned[:].rearrange("p s (j h) -> p s j h", h=SEG),
-                axis=AX.X,
-                op=ALU.max,
+                out=best[:], in_=turned[:].rearrange("p s (j h) -> p s j h", h=8), axis=AX.X, op=ALU.max
             )
-        nc.scalar.activation(out=result[:, :, 0:16], in_=best[:], func=ACT.Tanh)
+            nc.scalar.activation(out=result[:, s0:s1, 16 * c : 16 * (c + 1)], in_=best[:], func=ACT.Tanh)
         nc.sync.dma_start(out=out[0].rearrange("(m s) j -> m s j", s=4), in_=result[:])

@@ -33,9 +33,8 @@ def tile_attend_tok_headmax_topk_kernel(tc, qT, k_words, k_scales, hw, offs, out
 
         RAW_BYTES = PACK * HALF * 4
         offsets = sb.tile([P, N // 16], U16, name="offsets")
-        pool_scales = reused.tile([P, 2 * RAW_BYTES], U8, name="pool_scales", offset=0)
+        pool_scales = reused.tile([P, 2 * RAW_BYTES + 32], U8, name="pool_scales", offset=0)
         pool_words = sb.tile([P, T], U32, name="pool_words", align_bytes=64)
-        hw_cols = sb.tile([P, 2, 2], F32, name="hw_cols")
         raw = {}
 
         def load_q(c, o, tile):
@@ -56,7 +55,6 @@ def tile_attend_tok_headmax_topk_kernel(tc, qT, k_words, k_scales, hw, offs, out
         )
         for o in range(PASSES):
             load_q(0, o, sb.tile([P, PACK, HALF], F32, name="raw0%d" % o))
-        nc.sync.dma_start(out=hw_cols[:], in_=hw[0, 0, :].rearrange("(c p r) -> p c r", c=2, r=2))
 
         nc.vector.memset(pool_scales[32:64, 0:T].bitcast(I32), 0)
         nc.vector.memset(pool_scales[64:128, 0:T].bitcast(I32), 0)
@@ -78,14 +76,19 @@ def tile_attend_tok_headmax_topk_kernel(tc, qT, k_words, k_scales, hw, offs, out
             )
         for o in range(PASSES):
             load_q(1, o, reused.tile([P, PACK, HALF], F32, name="raw1%d" % o, offset=o * RAW_BYTES))
+        hw_cols = reused.tile([P, 2, 2], F32, name="hw_cols", offset=2 * RAW_BYTES)
+        nc.sync.dma_start(out=hw_cols[:], in_=hw[0, 0, :].rearrange("(c p r) -> p c r", c=2, r=2))
 
         got_words = sb.tile([P, N], U32, name="got_words", align_bytes=64)
         nc.vector.tensor_copy(got_words[:], pool_words[:].indirect(offsets[:]))
-        k_codes = []
         halves = got_words[:].bitcast(U16).rearrange("p (n o) -> p o n", o=PASSES)
-        for o in range(PASSES):
-            k_codes.append(sb.tile([P, N], U16, name="k_codes%d" % o, align_bytes=64))
+        k_codes = {}
+
+        def part_words(o, tag):
+            k_codes[o] = sb.tile([P, N], U16, name="k_codes", tag=tag, align_bytes=64)
             nc.vector.tensor_copy(out=k_codes[o][:], in_=halves[:, o, :])
+
+        part_words(0, "k_codes0")
 
         def weave(c, o, r, tag, engine):
             g = sb.tile([P, P, PACK], BF16, name="woven", tag=tag, align_bytes=64)
@@ -105,6 +108,8 @@ def tile_attend_tok_headmax_topk_kernel(tc, qT, k_words, k_scales, hw, offs, out
                 nc.vector.quantize_mx(
                     out=codes[:].bitcast(FP8X4), scales=scales[:], in_=woven[r][:].rearrange("p m j -> p (m j)")
                 )
+                if (c, o, r) == (0, 0, 0):
+                    part_words(1, "w0")
                 nc.tensor.matmul_mx(
                     out=acc[r][:],
                     lhsT=codes[:].bitcast(FP8X4),
@@ -123,7 +128,10 @@ def tile_attend_tok_headmax_topk_kernel(tc, qT, k_words, k_scales, hw, offs, out
         both = {}
         for c, s0, s1 in [(0, 0, 4), (1, 0, 2), (1, 2, 4)]:
             dealt = [acc[c][r][:].rearrange("p (m s) -> p s m", s=4)[:, s0:s1, :] for r in range(2)]
-            first = sb.tile([P, s1 - s0, P], F32, name="first", tag="first%d" % s0)
+            if c == 0:
+                first = reused.tile([P, s1 - s0, P], F32, name="first", offset=RAW_BYTES)
+            else:
+                first = sb.tile([P, s1 - s0, P], F32, name="first", tag="first%d" % s0)
             nc.scalar.activation(out=first[:], in_=dealt[0], func=ACT.Copy, scale=hw_cols[:, c, 0:1])
             larger = sb.tile(
                 [P, s1 - s0, P], F32, name="larger", tag=["w4", "larger10", "larger12"][c + s0 // 2], align_bytes=64

from contextlib import ExitStack

import concourse.mybir as mybir
from concourse.masks import make_identity

N, T, D, NQ, SEG = 512, 2048, 1024, 512, 16
P = 128
PACK = 4
PASSES = 2
HALF = 256

F32 = mybir.dt.float32
BF16 = mybir.dt.bfloat16
I32 = mybir.dt.int32
U32 = mybir.dt.uint32
U16 = mybir.dt.uint16
U8 = mybir.dt.uint8
FP8X4 = mybir.dt.float8_e4m3fn_x4
FP4X4 = mybir.dt.float4_e2m1fn_x4
ALU = mybir.AluOpType
ACT = mybir.ActivationFunctionType
AX = mybir.AxisListType

FLOPS = 2 * N * NQ * D


def tile_attend_tok_headmax_topk_kernel(tc, qT, k_words, k_scales, hw, offs, out):
    nc = tc.nc
    with ExitStack() as ctx:
        sb = ctx.enter_context(tc.tile_pool(name="sb", bufs=1))
        reused = ctx.enter_context(tc.tile_pool(name="reused", bufs=1))
        ps = ctx.enter_context(tc.psum_pool(name="ps", bufs=1))

        RAW_BYTES = PACK * HALF * 4
        offsets = sb.tile([P, N // 16], U16, name="offsets")
        pool_scales = reused.tile([P, 2 * RAW_BYTES + 32], U8, name="pool_scales", offset=0)
        pool_words = sb.tile([P, T], U32, name="pool_words", align_bytes=64)
        raw = {}

        def load_q(c, o, tile):
            raw[c, o] = tile
            nc.sync.dma_start(
                out=tile[:],
                in_=qT[0, 512 * o : 512 * (o + 1), HALF * c : HALF * (c + 1)].rearrange("(p j) w -> p j w", j=PACK),
            )

        nc.sync.dma_start(
            out=pool_scales[0:32, 0:T].bitcast(I32),
            in_=k_scales.bitcast(I32).rearrange("o f t -> f o t"),
        )
        nc.sync.dma_start(offsets[:], offs)
        nc.sync.dma_start(
            out=pool_words[:].bitcast(I32),
            in_=k_words.rearrange("v p t b -> p (v t b)").bitcast(I32),
        )
        for o in range(PASSES):
            load_q(0, o, sb.tile([P, PACK, HALF], F32, name="raw0%d" % o))

        nc.vector.memset(pool_scales[32:64, 0:T].bitcast(I32), 0)
        nc.vector.memset(pool_scales[64:128, 0:T].bitcast(I32), 0)
        warm = sb.tile([P, 1], F32, name="warm")
        warm_out = sb.tile([P, 1], F32, name="warm_out")
        nc.gpsimd.memset(warm[:], 0.0)
        nc.scalar.activation(out=warm_out[:], in_=warm[:], func=ACT.Tanh)
        k_planes = sb.tile([P, PASSES, N], U8, name="k_planes", align_bytes=64)
        nc.gpsimd.memset(k_planes[:].rearrange("p o n -> p (o n)").bitcast(I32), 0)
        ident = sb.tile([P, P], F32, name="ident")
        make_identity(nc, ident[:])

        got_scales = sb.tile([P, N], U8, name="got_scales", align_bytes=64)
        nc.vector.tensor_copy(got_scales[:], pool_scales[:, 0:T].indirect(offsets[:]))
        for Q in range(4):
            nc.sync.dma_start(
                out=k_planes[32 * Q : 32 * Q + 4, :, :].bitcast(I32),
                in_=got_scales[8 * Q : 8 * Q + 8, :].bitcast(I32),
            )
        for o in range(PASSES):
            load_q(1, o, reused.tile([P, PACK, HALF], F32, name="raw1%d" % o, offset=o * RAW_BYTES))
        hw_cols = reused.tile([P, 2, 2], F32, name="hw_cols", offset=2 * RAW_BYTES)
        nc.sync.dma_start(out=hw_cols[:], in_=hw[0, 0, :].rearrange("(c p r) -> p c r", c=2, r=2))

        got_words = sb.tile([P, N], U32, name="got_words", align_bytes=64)
        nc.vector.tensor_copy(got_words[:], pool_words[:].indirect(offsets[:]))
        halves = got_words[:].bitcast(U16).rearrange("p (n o) -> p o n", o=PASSES)
        k_codes = {}

        def part_words(o, tag):
            k_codes[o] = sb.tile([P, N], U16, name="k_codes", tag=tag, align_bytes=64)
            nc.vector.tensor_copy(out=k_codes[o][:], in_=halves[:, o, :])

        part_words(0, "k_codes0")

        def weave(c, o, r, tag, engine):
            g = sb.tile([P, P, PACK], BF16, name="woven", tag=tag, align_bytes=64)
            dst = g[:].rearrange("p (n i) j -> p n j i", i=4)
            src = raw[c, o][:].rearrange("p j (n i r) -> p r n j i", r=2, i=4)[:, r]
            if engine == "v":
                nc.vector.tensor_copy(out=dst, in_=src)
            else:
                nc.scalar.copy(out=dst, in_=src)
            return g

        def score(c, o, acc):
            woven = [weave(c, o, r, [["w0", "w1"], ["w1", "w2"], ["w2", "w3"], ["w3", "w4"]][2 * c + o][r], [["s", "s"], ["v", "s"], ["v", "s"], ["v", "s"]][2 * c + o][r]) for r in range(2)]
            for r in range(2):
                codes = sb.tile([P, P], U32, name="codes%d%d%d" % (c, o, r), align_bytes=64)
                scales = sb.tile([P, P], U8, name="scales%d%d%d" % (c, o, r), align_bytes=64)
                nc.vector.quantize_mx(
                    out=codes[:].bitcast(FP8X4), scales=scales[:], in_=woven[r][:].rearrange("p m j -> p (m j)")
                )
                if (c, o, r) == (0, 0, 0):
                    part_words(1, "w0")
                nc.tensor.matmul_mx(
                    out=acc[r][:],
                    lhsT=codes[:].bitcast(FP8X4),
                    lhsT_scale=scales[:],
                    rhs=k_codes[o][:].bitcast(FP4X4),
                    rhs_scale=k_planes[:, o, :],
                    start=(o == 0),
                    stop=(o == PASSES - 1),
                )

        acc = [[ps.tile([P, N], F32, name="acc", tag="acc%d%d" % (c, r)) for r in range(2)] for c in range(2)]
        for c in range(2):
            for o in range(PASSES):
                score(c, o, acc[c])

        both = {}
        for c, s0, s1 in [(0, 0, 4), (1, 0, 2), (1, 2, 4)]:
            dealt = [acc[c][r][:].rearrange("p (m s) -> p s m", s=4)[:, s0:s1, :] for r in range(2)]
            if c == 0:
                first = reused.tile([P, s1 - s0, P], F32, name="first", offset=RAW_BYTES)
            else:
                first = sb.tile([P, s1 - s0, P], F32, name="first", tag="first%d" % s0)
            nc.scalar.activation(out=first[:], in_=dealt[0], func=ACT.Copy, scale=hw_cols[:, c, 0:1])
            larger = sb.tile(
                [P, s1 - s0, P], F32, name="larger", tag=["w4", "larger10", "larger12"][c + s0 // 2], align_bytes=64
            )
            nc.vector.scalar_tensor_tensor(
                out=larger[:], in0=dealt[1], scalar=hw_cols[:, c, 1:2], in1=first[:], op0=ALU.mult, op1=ALU.max
            )
            for s in range(s0, s1):
                both[c, s] = larger[:, s - s0, :]
        result = sb.tile([P, 4, NQ // SEG], F32, name="result")
        for c, s0, s1 in [(0, 0, 4), (1, 0, 2), (1, 2, 4)]:
            best = sb.tile([P, s1 - s0, 16], F32, name="best", tag=["first2", "best10", "best12"][c + s0 // 2])
            turned = ps.tile([P, s1 - s0, P], F32, name="turned%d%d" % (c, s0))
            for s in range(s0, s1):
                nc.tensor.transpose(turned[:, s - s0, :], both[c, s], ident[:])
            nc.vector.tensor_reduce(
                out=best[:], in_=turned[:].rearrange("p s (j h) -> p s j h", h=8), axis=AX.X, op=ALU.max
            )
            nc.scalar.activation(out=result[:, s0:s1, 16 * c : 16 * (c + 1)], in_=best[:], func=ACT.Tanh)
        nc.sync.dma_start(out=out[0].rearrange("(m s) j -> m s j", s=4), in_=result[:])
